import numpy as np
import ml_dtypes


def mxq(x, axis, fmt="e4m3"):
    dtype, down = {"e4m3": (ml_dtypes.float8_e4m3fn, 7), "e5m2": (ml_dtypes.float8_e5m2, 14)}[fmt]
    v = np.moveaxis(np.asarray(x, np.float32).astype(ml_dtypes.bfloat16).astype(np.float64), axis, -1)
    blocks = v.reshape(v.shape[:-1] + (-1, 32))
    amax = np.abs(blocks).max(-1, keepdims=True)
    byte = np.maximum(np.where(amax > 0, np.frexp(amax)[1] - 1 + 127, 0) - down, 1)
    scale = np.exp2(byte - 127.0)
    codes = (blocks / scale).astype(np.float32).astype(dtype).astype(np.float64)
    return np.moveaxis((codes * scale).reshape(v.shape), -1, axis)


WIDE = False


def mx_kscale(k):
    if not WIDE:
        return np.ones(k)
    levels = np.array([10, -10, 5, -5, 0])
    if k % 512:
        return np.exp2(np.random.permutation(np.resize(levels, k // 32))).repeat(32)
    a = np.empty((k // 512, 16))
    for p in range(k // 512):
        a[p, :8] = np.random.permutation(np.resize(levels, 8))
        for g in range(8):
            far = levels[np.abs(levels - a[p, g]) >= 10]
            a[p, g + 8] = far[np.random.randint(len(far))]
    return np.exp2(a.ravel()).repeat(32)


def f64(x):
    return np.asarray(x).astype(np.float64)


def striped(idx):
    return np.tile(idx.reshape(-1, 16).T, (8, 1)).astype(np.uint16)


def unstriped(offs):
    return offs[:16].T.reshape(-1).astype(np.int64)


E2M1 = np.array([0.0, 0.5, 1.0, 1.5, 2.0, 3.0, 4.0, 6.0, -0.0, -0.5, -1.0, -1.5, -2.0, -3.0, -4.0, -6.0])


def pack_weight(w, fmt):
    k, n = w.shape
    w = f64(np.asarray(w, np.float32).astype(ml_dtypes.bfloat16)).reshape(k // 32, 32, n)
    amax = np.abs(w).max(1)
    if fmt == "e4m3":
        byte = np.frexp(amax)[1] - 1 + 127 - 7
    else:
        mant, ex = np.frexp(amax / 6.0)
        byte = np.where(mant > 0.5, ex, ex - 1) + 127
    byte = np.clip(np.where(amax > 0, byte, 1), 1, 254)
    scaled = (w * np.exp2(127.0 - byte)[:, None, :]).reshape(k, n).astype(np.float32)
    by_word = np.ascontiguousarray(scaled.reshape(k // 512, 128, 4, n).transpose(0, 1, 3, 2))
    if fmt == "e4m3":
        words = by_word.astype(ml_dtypes.float8_e4m3fn).view(np.uint8)
    else:
        c = by_word.astype(ml_dtypes.float4_e2m1fn).view(np.uint8) & 0xF
        words = (c[..., 0::2] | (c[..., 1::2] << 4)).reshape(k // 512, 128, 2 * n)
    return np.ascontiguousarray(words), np.ascontiguousarray(byte.astype(np.uint8).reshape(k // 512, 16, n))


def unpack_weight(words, scales, fmt):
    g, _, n = scales.shape
    words = np.ascontiguousarray(words).reshape(g, 128, n, -1)
    if fmt == "e4m3":
        vals = words.view(ml_dtypes.float8_e4m3fn).astype(np.float64)
    else:
        nib = np.empty((g, 128, n, 4), np.uint8)
        nib[..., 0::2] = words & 0xF
        nib[..., 1::2] = words >> 4
        vals = E2M1[nib]
    vals = vals * np.repeat(np.exp2(scales.astype(np.float64) - 127.0), 8, axis=1)[..., None]
    return vals.transpose(0, 1, 3, 2).reshape(g * 512, n)


def gelu(v):
    return 0.5 * v * (1.0 + np.tanh(np.sqrt(2.0 / np.pi) * (v + 0.044715 * v**3)))


def twice(P):
    return np.random.permutation(np.repeat(np.arange(P), 2))


def bf(x):
    return np.asarray(x, np.float32).astype(ml_dtypes.bfloat16)


def planes(Y):
    n, m = Y.shape
    b = f64(bf(Y)).reshape(n // 32, 32, m)
    amax = np.abs(b).max(1)
    byte = np.clip(np.where(amax > 0, np.frexp(amax)[1] - 1 + 127 - 7, 1), 1, 254)
    codes = (b * np.exp2(127.0 - byte)[:, None, :]).reshape(n, m).astype(np.float32).astype(ml_dtypes.float8_e4m3fn).view(np.uint8)
    words = codes.reshape(n // 512, 128, 4, m).transpose(0, 1, 3, 2)
    return np.ascontiguousarray(words), np.ascontiguousarray(byte.astype(np.uint8).reshape(n // 512, 16, m))


K, T, S, P, H = 1536, 4096, 1024, 512, 1024


def setup_inputs():
    n = np.random.standard_normal
    s = mx_kscale(K)[:, None]
    u = mx_kscale(H)[:, None]
    e = np.exp(0.8 * n(H))
    d = {}
    d["tab_words"], d["tab_scales"] = pack_weight(n((K, T)) * s, "e4m3")
    d["offs"] = striped(np.random.permutation(T)[:S])
    d["w1"] = (n((K, H)) / K ** 0.5 / s * u.T).astype(np.float32)
    d["pos1"] = striped(np.random.permutation(S)[:P])
    d["pos2"] = striped(np.random.permutation(S)[:P])
    d["w4_words"], d["w4_scales"] = pack_weight(1.2 * n((H, H)) / H ** 0.5 / u * e[None, :], "e2m1")
    d["pos3"] = striped(twice(P))
    d["gh"] = (e / u[:, 0]).astype(np.float32)
    return d


def reference(tab_words, tab_scales, offs, w1, pos1, pos2, w4_words, w4_scales, pos3, gh):
    v = unpack_weight(tab_words, tab_scales, "e4m3")[:, unstriped(offs)]
    w4 = unpack_weight(w4_words, w4_scales, "e2m1")
    h = mxq(f64(w1), 0, "e4m3").T @ v
    h1 = h[:, unstriped(pos1)]
    h2 = h[:, unstriped(pos2)]
    z = np.sqrt(np.square(h1) + np.square(h2))
    b = w4.T @ mxq(z, 0, "e4m3")
    up = b[:, unstriped(pos3)]
    act = up / (1.0 + np.exp(-up))
    y = f64(gh)[:, None] * h + act
    words, scales = planes(y)
    return y, words, scales

@@ -1,0 +1,332 @@
+from contextlib import ExitStack
+
+import concourse.mybir as mybir
+
+K, T, S, M, H = 1536, 4096, 1024, 512, 1024
+FLOPS = 2 * K * H * S + 2 * H * H * M
+
+F32 = mybir.dt.float32
+BF16 = mybir.dt.bfloat16
+I32 = mybir.dt.int32
+U32 = mybir.dt.uint32
+U16 = mybir.dt.uint16
+U8 = mybir.dt.uint8
+FP8X4 = mybir.dt.float8_e4m3fn_x4
+FP4X4 = mybir.dt.float4_e2m1fn_x4
+ACT = mybir.ActivationFunctionType
+ALU = mybir.AluOpType
+
+P = 128
+PACK = 4
+KP = P * PACK
+BANK = 512
+PASSES = K // KP
+GROUPS = H // KP
+TILES = GROUPS * PACK
+
+
+def tile_list_blast_window_features_kernel(
+    tc, tab_words, tab_scales, offs, w1, pos1, pos2, w4_words, w4_scales, pos3, gh, out_0, out_1, out_2
+):
+    nc = tc.nc
+    with ExitStack() as ctx:
+        lists = ctx.enter_context(tc.tile_pool(name="lists", bufs=1))
+        keep = ctx.enter_context(tc.tile_pool(name="keep", bufs=1))
+        psum = ctx.enter_context(tc.psum_pool(name="psum", bufs=8))
+
+        def big(shape, dtype, name):
+            return keep.tile(shape, dtype, name=name, tag="big", bufs=2, align_bytes=64)
+
+        def mid(shape, dtype, name):
+            return keep.tile(shape, dtype, name=name, tag="mid", bufs=2, align_bytes=64)
+
+        def picked(name, early=False):
+            if early:
+                return keep.tile([P, S], F32, name=name, tag="early", bufs=4, align_bytes=64)
+            return keep.tile([P, S], F32, name=name, tag="picked", bufs=6, align_bytes=64)
+
+        def bank(name):
+            return psum.tile([P, BANK], F32, name=name, tag="bank")
+
+        offs_sb = lists.tile([P, S // 16], U16, name="offs_sb")
+        pos1_sb = lists.tile([P, M // 16], U16, name="pos1_sb")
+        pos2_sb = lists.tile([P, M // 16], U16, name="pos2_sb")
+        pos3_sb = lists.tile([P, S // 16], U16, name="pos3_sb")
+        gh_sb = lists.tile([P, GROUPS, PACK], F32, name="gh_sb")
+        warm = lists.tile([P, 8], F32, name="warm")
+
+        nc.vector.memset(warm[:], 1.0)
+        nc.scalar.activation(warm[:, 0:1], warm[:, 1:2], ACT.Sqrt)
+
+        ts = keep.tile([P, T], U8, name="ts", align_bytes=64)
+        nc.vector.memset(ts[:].bitcast(I32), 0)
+        for q in range(4):
+            nc.gpsimd.dma_start(
+                ts[32 * q : 32 * q + 4 * PASSES, :].bitcast(I32), tab_scales[:, 4 * q : 4 * q + 4, :].bitcast(I32)
+            )
+
+        wq = {}
+        ws = {}
+
+        def load_w1(g, a, ring, pieces=1):
+            raw = ring([P, PACK, KP], F32, "wraw%d%d" % (g, a))
+            src = w1[a * KP : (a + 1) * KP, g * KP : (g + 1) * KP].rearrange("(p j) c -> p j c", j=PACK)
+            for c in range(0, KP, KP // pieces):
+                nc.sync.dma_start(raw[:, :, c : c + KP // pieces], src[:, :, c : c + KP // pieces])
+            return raw
+
+        def round_w1(g, a, raw, split):
+            grouped = keep.tile([P, PACK, P, PACK], BF16, name="wg%d%d" % (g, a), tag="wg", bufs=3, align_bytes=64)
+            src = raw[:].rearrange("p j (m t) -> p m j t", t=PACK)
+            dst = grouped[:].rearrange("p t m j -> p m j t")
+            for c in range(0, P - split, 32):
+                nc.scalar.copy(dst[:, c : min(c + 32, P - split)], src[:, c : min(c + 32, P - split)])
+            if split > 0:
+                nc.vector.tensor_copy(dst[:, P - split : P], src[:, P - split : P])
+            return grouped
+
+        def quant_w1(g, a, grouped, cuts=(0, PACK)):
+            wq[g, a] = keep.tile([P, KP], U32, name="wq%d%d" % (g, a), align_bytes=64)
+            ws[g, a] = keep.tile([P, KP], U8, name="ws%d%d" % (g, a), align_bytes=64)
+            for lo, hi in zip(cuts[:-1], cuts[1:]):
+                nc.vector.quantize_mx(
+                    out=wq[g, a][:, lo * P : hi * P].bitcast(FP8X4),
+                    scales=ws[g, a][:, lo * P : hi * P],
+                    in_=grouped[:, lo:hi].rearrange("p t m j -> p (t m j)"),
+                )
+
+        def load_w4():
+            words = mid([P, GROUPS, 2 * H], U8, "w4raw")
+            nc.sync.dma_start(words[:].bitcast(I32), w4_words.rearrange("a p c -> p a c").bitcast(I32))
+            scales = mid([P, GROUPS, H], U8, "w4sraw")
+            nc.gpsimd.memset(scales[:].bitcast(I32), 0)
+            for q in range(4):
+                nc.sync.dma_start(
+                    scales[32 * q : 32 * q + 4].bitcast(I32),
+                    w4_scales[:, 4 * q : 4 * q + 4, :].rearrange("a r c -> r a c").bitcast(I32),
+                )
+            return words, scales
+
+        w4d = {}
+        w4s = {}
+
+        def deal_w4(g):
+            w4d[g] = keep.tile([P, GROUPS, 2 * KP], U8, name="w4d%d" % g, align_bytes=64)
+            nc.vector.tensor_copy(
+                w4d[g][:].bitcast(U16).rearrange("p a (t q) -> p a q t", t=PACK),
+                w4raw[:, :, g * 2 * KP : (g + 1) * 2 * KP].bitcast(U16).rearrange("p a (q t) -> p a q t", t=PACK),
+            )
+            w4s[g] = keep.tile([P, GROUPS, KP], U8, name="w4s%d" % g, align_bytes=64)
+            nc.vector.tensor_copy(
+                w4s[g][:].rearrange("p a (t q) -> p a q t", t=PACK),
+                w4sraw[:, :, g * KP : (g + 1) * KP].rearrange("p a (q t) -> p a q t", t=PACK),
+            )
+
+        v = [keep.tile([P, S], U32, name="v%d" % a, align_bytes=64) for a in range(PASSES)]
+        vs = keep.tile([P, S], U8, name="vs", align_bytes=64)
+
+        def stage1_pass(acc, g, t, a, half):
+            cols = slice(half * BANK, (half + 1) * BANK)
+            rows = slice(t * P, (t + 1) * P)
+            nc.tensor.matmul_mx(
+                out=acc[:],
+                lhsT=wq[g, a][:, rows].bitcast(FP8X4),
+                lhsT_scale=ws[g, a][:, rows],
+                rhs=v[a][:, cols].bitcast(FP8X4),
+                rhs_scale=vs[4 * a :, cols],
+                start=(a == 0),
+                stop=(a == PASSES - 1),
+            )
+
+        accs = {}
+        for a in range(PASSES):
+            tw = big([P, T], I32, "tw%d" % a)
+            nc.sync.dma_start(tw[:], tab_words[a].rearrange("p t i -> p (t i)").bitcast(I32))
+            if a == 0:
+                nc.sync.dma_start(offs_sb[:], offs)
+            nc.vector.tensor_copy(v[a][:], tw[:].bitcast(U32).indirect(offs_sb[:]))
+            if a == 0:
+                nc.vector.tensor_copy(vs[:], ts[:].indirect(offs_sb[:]))
+            if a < PASSES - 1:
+                quant_w1(0, a, round_w1(0, a, load_w1(0, a, mid), 0))
+            else:
+                quant_w1(0, a, round_w1(0, a, load_w1(0, a, mid, 2), P // 2), (0, 1, 2, PACK))
+            if a == 1:
+                nc.sync.dma_start(pos1_sb[:], pos1)
+                nc.sync.dma_start(pos2_sb[:], pos2)
+                nc.sync.dma_start(pos3_sb[:], pos3)
+                nc.sync.dma_start(gh_sb[:], gh.rearrange("(g p t) -> p g t", g=GROUPS, t=PACK))
+            for t in range(PACK):
+                for half in range(2):
+                    if a == 0:
+                        accs[t, half] = bank("acc0%d%d" % (t, half))
+                    stage1_pass(accs[t, half], 0, t, a, half)
+        raws = [load_w1(1, a, big if a == 0 else mid) for a in range(PASSES)]
+        w4raw, w4sraw = load_w4()
+
+        h = [keep.tile([P, S], F32, name="h%d" % i, align_bytes=64) for i in range(TILES)]
+        zsum = [keep.tile([P, PACK, M], F32, name="zsum%d" % g, align_bytes=64) for g in range(GROUPS)]
+        zb = [keep.tile([P, M, PACK], BF16, name="zb%d" % g, align_bytes=64) for g in range(GROUPS)]
+        zq = [keep.tile([P, M], U32, name="zq%d" % g, align_bytes=64) for g in range(GROUPS)]
+        zs = [keep.tile([P, M], U8, name="zs%d" % g, align_bytes=64) for g in range(GROUPS)]
+
+        def evacuate_h(g, t):
+            for half in range(2):
+                dst = h[PACK * g + t][:, half * BANK : (half + 1) * BANK]
+                if (g, t, half) == (0, 0, 1):
+                    nc.vector.tensor_copy(dst, accs[t, half][:])
+                else:
+                    nc.scalar.copy(dst, accs[t, half][:])
+
+        def pick_pairs(g, t, lo, hi):
+            n = hi - lo
+            pair = picked("pair%d%d%d" % (g, t, lo), PACK * g + t < 0)
+            win = h[PACK * g + t]
+            nc.vector.tensor_copy(pair[:, 0:n], win[:].indirect(pos1_sb[:, lo // 16 : hi // 16]))
+            nc.vector.tensor_copy(pair[:, n : 2 * n], win[:].indirect(pos2_sb[:, lo // 16 : hi // 16]))
+            return pair
+
+        def add_pairs(g, t, lo, hi, pair):
+            n = hi - lo
+            nc.vector.tensor_tensor(zsum[g][:, t, lo:hi], pair[:, 0:n], pair[:, n : 2 * n], ALU.add)
+
+        def root(g, lo, hi):
+            nc.scalar.activation(
+                zb[g][:, lo:hi, :].rearrange("p (c i) t -> p c t i", i=4),
+                zsum[g][:, :, lo:hi].rearrange("p t (c i) -> p c t i", i=4),
+                ACT.Sqrt,
+            )
+
+        def quant_z(g, lo, hi):
+            nc.vector.quantize_mx(
+                out=zq[g][:, lo:hi].bitcast(FP8X4), scales=zs[g][:, lo:hi], in_=zb[g][:, lo:hi, :].rearrange("p m t -> p (m t)")
+            )
+
+        y = [big([P, PACK, S], F32, "y%d" % g) for g in range(GROUPS)]
+
+        def scale_h(i):
+            nc.gpsimd.tensor_scalar(y[i // PACK][:, i % PACK, :], h[i][:], gh_sb[:, i // PACK, i % PACK : i % PACK + 1], 0.0, ALU.mult, ALU.add)
+
+        on_pool = []
+        steps = [(0, t, 0, M) for t in range(PACK)] + [(1, 0, 0, M), (1, 1, 0, M)] + [(1, 2, 0, 256), (1, 3, 0, 256), (1, 2, 256, M), (1, 3, 256, M)]
+        w_split = [0, 0, 0]
+        def finish_pairs(g, t, lo, hi, pair):
+            nc.scalar.activation(pair[:, 0 : 2 * (hi - lo)], pair[:, 0 : 2 * (hi - lo)], ACT.Square)
+            add_pairs(g, t, lo, hi, pair)
+            if t == PACK - 1:
+                for c in range(lo, hi, 256):
+                    root(g, c, min(hi, c + 256))
+                    quant_z(g, c, min(hi, c + 256))
+
+        lag = 1
+        ahead = 1
+        picks = []
+        ready = 0
+        for n, (g, t, lo, hi) in enumerate(steps):
+            while ready < min(TILES, n + ahead + 1):
+                if ready >= PACK:
+                    for half in range(2):
+                        accs[ready % PACK, half] = bank("acc1%d%d" % (ready % PACK, half))
+                        for a in range(PASSES):
+                            stage1_pass(accs[ready % PACK, half], 1, ready % PACK, a, half)
+                evacuate_h(ready // PACK, ready % PACK)
+
+                ready = ready + 1
+            picks.append((g, t, lo, hi, pick_pairs(g, t, lo, hi)))
+            if n < PASSES:
+                quant_w1(1, n, round_w1(1, n, raws[n], w_split[n]))
+            if n >= lag:
+                finish_pairs(*picks[n - lag])
+            if n in on_pool:
+                scale_h(n)
+            if n in [5, 6]:
+                deal_w4([5, 6].index(n))
+
+        for item in picks[len(steps) - lag :]:
+            finish_pairs(*item)
+        nc.scalar.activation(warm[:, 2:3], zb[1][:, M - 1, 0:1], ACT.Silu)
+
+        bt = keep.tile([P, TILES * M], F32, name="bt", align_bytes=64)
+
+        def stage2(i):
+            acc = bank("acc2%d" % i)
+            pieces = [(0, 0, M)] + ([(1, c, c + P) for c in range(0, M, P)] if i < 0 else [(1, 0, M)])
+            for k, (a, lo, hi) in enumerate(pieces):
+                nc.tensor.matmul_mx(
+                    out=acc[:, lo:hi],
+                    lhsT=w4d[i // PACK][:, a, 2 * P * (i % PACK) : 2 * P * (i % PACK + 1)].bitcast(FP4X4),
+                    lhsT_scale=w4s[i // PACK][:, a, P * (i % PACK) : P * (i % PACK + 1)],
+                    rhs=zq[a][:, lo:hi].bitcast(FP8X4),
+                    rhs_scale=zs[a][:, lo:hi],
+                    start=(k == 0),
+                    stop=(k == len(pieces) - 1),
+                )
+            base = (TILES - 1 - i) * M
+            if i == 0:
+                nc.vector.tensor_copy(bt[:, base : base + M], acc[:])
+            else:
+                nc.scalar.copy(bt[:, base : base + M], acc[:])
+
+        yq = [keep.tile([P, S], I32, name="yq%d" % g, align_bytes=64) for g in range(GROUPS)]
+        ys = [keep.tile([P, S], U8, name="ys%d" % g, align_bytes=64) for g in range(GROUPS)]
+
+        def pick_up(g, t, lo, hi):
+            i = PACK * g + t
+            base = (TILES - 1 - i) * M
+            up = picked("up%d%d%d" % (g, t, lo))
+            piece = min(hi - lo, 256 << min(i, 2))
+            width = max(M, 3 * piece // 2)
+            for c in range(lo, hi, piece):
+                nc.vector.tensor_copy(
+                    up[:, c - lo : c - lo + piece], bt[:, base : base + width].indirect(pos3_sb[:, c // 16 : (c + piece) // 16])
+                )
+            nc.scalar.activation(up[:, 0 : hi - lo], up[:, 0 : hi - lo], ACT.Silu)
+            return up
+
+        def combine(g, t, lo, hi, up):
+            i = PACK * g + t
+            if i in on_pool:
+                nc.gpsimd.tensor_tensor(y[g][:, t, lo:hi], y[g][:, t, lo:hi], up[:, 0 : hi - lo], ALU.add)
+            else:
+                nc.vector.scalar_tensor_tensor(
+                    y[g][:, t, lo:hi], h[i][:, lo:hi], gh_sb[:, g, t : t + 1], up[:, 0 : hi - lo], ALU.mult, ALU.add
+                )
+
+        def round_y(g, lo, hi, on_vector):
+            yb = keep.tile([P, hi - lo, PACK], BF16, name="yb%d%d" % (g, lo), tag="wg", bufs=3, align_bytes=64)
+            dst = yb[:].rearrange("p (c i) t -> p c t i", i=4)
+            src = y[g][:, :, lo:hi].rearrange("p t (c i) -> p c t i", i=4)
+            if on_vector:
+                nc.vector.tensor_copy(dst, src)
+            else:
+                nc.scalar.copy(dst, src)
+            nc.sync.dma_start(out_0[g * KP : (g + 1) * KP, lo:hi].rearrange("(p t) c -> p t c", t=PACK), y[g][:, :, lo:hi])
+            return yb
+
+        def quant_y(g, lo, hi, yb):
+            nc.vector.quantize_mx(
+                out=yq[g][:, lo:hi].bitcast(FP8X4), scales=ys[g][:, lo:hi], in_=yb[:].rearrange("p m t -> p (m t)")
+            )
+            nc.sync.dma_start(out_1[g].rearrange("p m t -> p (m t)").bitcast(I32)[:, lo:hi], yq[g][:, lo:hi])
+            if hi == S:
+                for q in range(4):
+                    nc.sync.dma_start(out_2[g, 4 * q : 4 * q + 4, :].bitcast(I32), ys[g][32 * q : 32 * q + 4, :].bitcast(I32))
+
+        steps = [(g, t, lo, hi) for g, cuts in ((0, (0, 512, S)), (1, (0, 512, 768, S))) for lo, hi in zip(cuts[:-1], cuts[1:]) for t in range(PACK)]
+        stage2(0)
+
+        stage2(1)
+        pending = None
+        for n, (g, t, lo, hi) in enumerate(steps):
+            up = pick_up(g, t, lo, hi)
+            if n + 2 < TILES:
+                stage2(n + 2)
+            if pending is not None:
+                combine(*pending)
+                pg, pt, plo, phi = pending[:4]
+                if pt == PACK - 1:
+                    for c in range(plo, phi, 256):
+                        quant_y(pg, c, min(c + 256, phi), round_y(pg, c, min(c + 256, phi), False))
+            pending = (g, t, lo, hi, up)
+        combine(*pending)
+        quant_y(1, pending[2], S, round_y(1, pending[2], S, True))

@@ -188,7 +188,7 @@ def tile_list_blast_window_features_kernel(
 
         def add_pairs(g, t, lo, hi, pair):
             n = hi - lo
-            nc.vector.tensor_tensor(zsum[g][:, t, lo:hi], pair[:, 0:n], pair[:, n : 2 * n], ALU.add)
+            nc.gpsimd.tensor_tensor(zsum[g][:, t, lo:hi], pair[:, 0:n], pair[:, n : 2 * n], ALU.add)
 
         def root(g, lo, hi):
             nc.scalar.activation(
@@ -207,9 +207,9 @@ def tile_list_blast_window_features_kernel(
         def scale_h(i):
             nc.gpsimd.tensor_scalar(y[i // PACK][:, i % PACK, :], h[i][:], gh_sb[:, i // PACK, i % PACK : i % PACK + 1], 0.0, ALU.mult, ALU.add)
 
-        on_pool = []
+        on_pool = [0,1,2,3,4,5]
         steps = [(0, t, 0, M) for t in range(PACK)] + [(1, 0, 0, M), (1, 1, 0, M)] + [(1, 2, 0, 256), (1, 3, 0, 256), (1, 2, 256, M), (1, 3, 256, M)]
-        w_split = [0, 0, 0]
+        w_split = [0, 32, 64]
         def finish_pairs(g, t, lo, hi, pair):
             nc.scalar.activation(pair[:, 0 : 2 * (hi - lo)], pair[:, 0 : 2 * (hi - lo)], ACT.Square)
             add_pairs(g, t, lo, hi, pair)

@@ -34,16 +34,17 @@ def tile_list_blast_window_features_kernel(
         keep = ctx.enter_context(tc.tile_pool(name="keep", bufs=1))
         psum = ctx.enter_context(tc.psum_pool(name="psum", bufs=8))
 
+        def held(shape, dtype, name):
+            return keep.tile(shape, dtype, name=name, align_bytes=64)
+
         def big(shape, dtype, name):
-            return keep.tile(shape, dtype, name=name, tag="big", bufs=2, align_bytes=64)
+            return keep.tile(shape, dtype, name=name, tag="big", bufs=3, align_bytes=64)
 
-        def mid(shape, dtype, name):
-            return keep.tile(shape, dtype, name=name, tag="mid", bufs=2, align_bytes=64)
+        def rounded(shape, name):
+            return keep.tile(shape, BF16, name=name, tag="rounded", bufs=3, align_bytes=64)
 
-        def picked(name, early=False):
-            if early:
-                return keep.tile([P, S], F32, name=name, tag="early", bufs=4, align_bytes=64)
-            return keep.tile([P, S], F32, name=name, tag="picked", bufs=6, align_bytes=64)
+        def picked(name):
+            return keep.tile([P, S], F32, name=name, tag="picked", bufs=8, align_bytes=64)
 
         def bank(name):
             return psum.tile([P, BANK], F32, name=name, tag="bank")
@@ -58,36 +59,41 @@ def tile_list_blast_window_features_kernel(
         nc.vector.memset(warm[:], 1.0)
         nc.scalar.activation(warm[:, 0:1], warm[:, 1:2], ACT.Sqrt)
 
-        ts = keep.tile([P, T], U8, name="ts", align_bytes=64)
+        ts = held([P, T], U8, "ts")
         nc.vector.memset(ts[:].bitcast(I32), 0)
+        w4sraw = held([P, GROUPS, H], U8, "w4sraw")
+        nc.vector.memset(w4sraw[:].bitcast(I32), 0)
         for q in range(4):
             nc.gpsimd.dma_start(
                 ts[32 * q : 32 * q + 4 * PASSES, :].bitcast(I32), tab_scales[:, 4 * q : 4 * q + 4, :].bitcast(I32)
             )
 
-        wq = {}
-        ws = {}
+        def load_table(a):
+            tw = big([P, T], I32, "tw%d" % a)
+            nc.sync.dma_start(tw[:], tab_words[a].rearrange("p t i -> p (t i)").bitcast(I32))
+            return tw
 
-        def load_w1(g, a, ring, pieces=1):
-            raw = ring([P, PACK, KP], F32, "wraw%d%d" % (g, a))
+        def load_w1(g, a, pieces=1):
+            raw = big([P, PACK, KP], F32, "wraw%d%d" % (g, a))
             src = w1[a * KP : (a + 1) * KP, g * KP : (g + 1) * KP].rearrange("(p j) c -> p j c", j=PACK)
             for c in range(0, KP, KP // pieces):
                 nc.sync.dma_start(raw[:, :, c : c + KP // pieces], src[:, :, c : c + KP // pieces])
             return raw
 
-        def round_w1(g, a, raw, split):
-            grouped = keep.tile([P, PACK, P, PACK], BF16, name="wg%d%d" % (g, a), tag="wg", bufs=3, align_bytes=64)
+        wq = {}
+        ws = {}
+
+        def quant_w1(g, a, raw, on_vector, cuts=(0, PACK)):
+            grouped = rounded([P, PACK, P, PACK], "wg%d%d" % (g, a))
             src = raw[:].rearrange("p j (m t) -> p m j t", t=PACK)
             dst = grouped[:].rearrange("p t m j -> p m j t")
-            for c in range(0, P - split, 32):
-                nc.scalar.copy(dst[:, c : min(c + 32, P - split)], src[:, c : min(c + 32, P - split)])
-            if split > 0:
-                nc.vector.tensor_copy(dst[:, P - split : P], src[:, P - split : P])
-            return grouped
-
-        def quant_w1(g, a, grouped, cuts=(0, PACK)):
-            wq[g, a] = keep.tile([P, KP], U32, name="wq%d%d" % (g, a), align_bytes=64)
-            ws[g, a] = keep.tile([P, KP], U8, name="ws%d%d" % (g, a), align_bytes=64)
+            for c in range(0, P - on_vector, 32):
+                hi = min(c + 32, P - on_vector)
+                nc.scalar.copy(dst[:, c:hi], src[:, c:hi])
+            if on_vector > 0:
+                nc.vector.tensor_copy(dst[:, P - on_vector : P], src[:, P - on_vector : P])
+            wq[g, a] = held([P, KP], U32, "wq%d%d" % (g, a))
+            ws[g, a] = held([P, KP], U8, "ws%d%d" % (g, a))
             for lo, hi in zip(cuts[:-1], cuts[1:]):
                 nc.vector.quantize_mx(
                     out=wq[g, a][:, lo * P : hi * P].bitcast(FP8X4),
@@ -95,41 +101,18 @@ def tile_list_blast_window_features_kernel(
                     in_=grouped[:, lo:hi].rearrange("p t m j -> p (t m j)"),
                 )
 
-        def load_w4():
-            words = mid([P, GROUPS, 2 * H], U8, "w4raw")
-            nc.sync.dma_start(words[:].bitcast(I32), w4_words.rearrange("a p c -> p a c").bitcast(I32))
-            scales = mid([P, GROUPS, H], U8, "w4sraw")
-            nc.gpsimd.memset(scales[:].bitcast(I32), 0)
-            for q in range(4):
-                nc.sync.dma_start(
-                    scales[32 * q : 32 * q + 4].bitcast(I32),
-                    w4_scales[:, 4 * q : 4 * q + 4, :].rearrange("a r c -> r a c").bitcast(I32),
-                )
-            return words, scales
+        v = [held([P, S], U32, "v%d" % a) for a in range(PASSES)]
+        vs = held([P, S], U8, "vs")
+        accs = {}
 
-        w4d = {}
-        w4s = {}
-
-        def deal_w4(g):
-            w4d[g] = keep.tile([P, GROUPS, 2 * KP], U8, name="w4d%d" % g, align_bytes=64)
-            nc.vector.tensor_copy(
-                w4d[g][:].bitcast(U16).rearrange("p a (t q) -> p a q t", t=PACK),
-                w4raw[:, :, g * 2 * KP : (g + 1) * 2 * KP].bitcast(U16).rearrange("p a (q t) -> p a q t", t=PACK),
-            )
-            w4s[g] = keep.tile([P, GROUPS, KP], U8, name="w4s%d" % g, align_bytes=64)
-            nc.vector.tensor_copy(
-                w4s[g][:].rearrange("p a (t q) -> p a q t", t=PACK),
-                w4sraw[:, :, g * KP : (g + 1) * KP].rearrange("p a (q t) -> p a q t", t=PACK),
-            )
-
-        v = [keep.tile([P, S], U32, name="v%d" % a, align_bytes=64) for a in range(PASSES)]
-        vs = keep.tile([P, S], U8, name="vs", align_bytes=64)
-
-        def stage1_pass(acc, g, t, a, half):
+        def stage1_pass(i, a, half):
+            g, t = divmod(i, PACK)
+            if a == 0:
+                accs[i, half] = bank("acc1_%d%d" % (i, half))
             cols = slice(half * BANK, (half + 1) * BANK)
             rows = slice(t * P, (t + 1) * P)
             nc.tensor.matmul_mx(
-                out=acc[:],
+                out=accs[i, half][:],
                 lhsT=wq[g, a][:, rows].bitcast(FP8X4),
                 lhsT_scale=ws[g, a][:, rows],
                 rhs=v[a][:, cols].bitcast(FP8X4),
@@ -138,172 +121,191 @@ def tile_list_blast_window_features_kernel(
                 stop=(a == PASSES - 1),
             )
 
-        accs = {}
+        w4raw = held([P, GROUPS, 2 * H], U8, "w4raw")
+        w4d = held([P, GROUPS, 2 * H], U8, "w4d")
+        w4s = held([P, GROUPS, H], U8, "w4s")
+
         for a in range(PASSES):
-            tw = big([P, T], I32, "tw%d" % a)
-            nc.sync.dma_start(tw[:], tab_words[a].rearrange("p t i -> p (t i)").bitcast(I32))
+            tw = load_table(a)
             if a == 0:
                 nc.sync.dma_start(offs_sb[:], offs)
-            nc.vector.tensor_copy(v[a][:], tw[:].bitcast(U32).indirect(offs_sb[:]))
-            if a == 0:
-                nc.vector.tensor_copy(vs[:], ts[:].indirect(offs_sb[:]))
-            if a < PASSES - 1:
-                quant_w1(0, a, round_w1(0, a, load_w1(0, a, mid), 0))
-            else:
-                quant_w1(0, a, round_w1(0, a, load_w1(0, a, mid, 2), P // 2), (0, 1, 2, PACK))
             if a == 1:
+                for q in range(4):
+                    nc.sync.dma_start(
+                        w4sraw[32 * q : 32 * q + 4].bitcast(I32),
+                        w4_scales[:, 4 * q : 4 * q + 4, :].rearrange("a r c -> r a c").bitcast(I32),
+                    )
+            last = a == PASSES - 1
+            raw = load_w1(0, a, 2 if last else 1)
+            if a == 0:
+                nc.sync.dma_start(w4raw[:].bitcast(I32), w4_words.rearrange("a p c -> p a c").bitcast(I32))
                 nc.sync.dma_start(pos1_sb[:], pos1)
                 nc.sync.dma_start(pos2_sb[:], pos2)
                 nc.sync.dma_start(pos3_sb[:], pos3)
                 nc.sync.dma_start(gh_sb[:], gh.rearrange("(g p t) -> p g t", g=GROUPS, t=PACK))
-            for t in range(PACK):
+            nc.vector.tensor_copy(v[a][:], tw[:].bitcast(U32).indirect(offs_sb[:]))
+            if a == 0:
+                nc.vector.tensor_copy(vs[:], ts[:].indirect(offs_sb[:]))
+            if last:
+                quant_w1(0, a, raw, P // 2, (0, 1, 2, PACK))
+            else:
+                quant_w1(0, a, raw, 0)
+            if a == 0:
+                nc.vector.tensor_copy(
+                    w4d[:].bitcast(U16).rearrange("p a (g t q) -> p (a g) q t", g=GROUPS, t=PACK),
+                    w4raw[:].bitcast(U16).rearrange("p a (g q t) -> p (a g) q t", g=GROUPS, t=PACK),
+                )
+            if a == 1:
+                nc.vector.tensor_copy(
+                    w4s[:].rearrange("p a (g t q) -> p (a g) q t", g=GROUPS, t=PACK),
+                    w4sraw[:].rearrange("p a (g q t) -> p (a g) q t", g=GROUPS, t=PACK),
+                )
+            for i in range(PACK):
                 for half in range(2):
-                    if a == 0:
-                        accs[t, half] = bank("acc0%d%d" % (t, half))
-                    stage1_pass(accs[t, half], 0, t, a, half)
-        raws = [load_w1(1, a, big if a == 0 else mid) for a in range(PASSES)]
-        w4raw, w4sraw = load_w4()
+                    stage1_pass(i, a, half)
+        raws = [load_w1(1, a) for a in range(PASSES)]
 
-        h = [keep.tile([P, S], F32, name="h%d" % i, align_bytes=64) for i in range(TILES)]
-        zsum = [keep.tile([P, PACK, M], F32, name="zsum%d" % g, align_bytes=64) for g in range(GROUPS)]
-        zb = [keep.tile([P, M, PACK], BF16, name="zb%d" % g, align_bytes=64) for g in range(GROUPS)]
-        zq = [keep.tile([P, M], U32, name="zq%d" % g, align_bytes=64) for g in range(GROUPS)]
-        zs = [keep.tile([P, M], U8, name="zs%d" % g, align_bytes=64) for g in range(GROUPS)]
+        h = [held([P, S], F32, "h%d" % i) for i in range(TILES)]
+        zsum = [held([P, PACK, M], F32, "zsum%d" % g) for g in range(GROUPS)]
+        zb = [held([P, M, PACK], BF16, "zb%d" % g) for g in range(GROUPS)]
+        zq = [held([P, M], U32, "zq%d" % g) for g in range(GROUPS)]
+        zs = [held([P, M], U8, "zs%d" % g) for g in range(GROUPS)]
+        y = [big([P, PACK, S], F32, "y%d" % g) for g in range(GROUPS)]
+        pool_cols = [0] * TILES
 
-        def evacuate_h(g, t):
+        def evacuate_h(i):
             for half in range(2):
-                dst = h[PACK * g + t][:, half * BANK : (half + 1) * BANK]
-                if (g, t, half) == (0, 0, 1):
-                    nc.vector.tensor_copy(dst, accs[t, half][:])
+                if i >= PACK:
+                    for a in range(PASSES):
+                        stage1_pass(i, a, half)
+                dst = h[i][:, half * BANK : (half + 1) * BANK]
+                if (i, half) == (0, 1):
+                    nc.vector.tensor_copy(dst, accs[i, half][:])
                 else:
-                    nc.scalar.copy(dst, accs[t, half][:])
+                    nc.scalar.copy(dst, accs[i, half][:])
 
-        def pick_pairs(g, t, lo, hi):
+        pairs = {}
+
+        def pick_pairs(i, lo, hi):
             n = hi - lo
-            pair = picked("pair%d%d%d" % (g, t, lo), PACK * g + t < 0)
-            win = h[PACK * g + t]
-            nc.vector.tensor_copy(pair[:, 0:n], win[:].indirect(pos1_sb[:, lo // 16 : hi // 16]))
-            nc.vector.tensor_copy(pair[:, n : 2 * n], win[:].indirect(pos2_sb[:, lo // 16 : hi // 16]))
-            return pair
+            pair = picked("pair%d_%d" % (i, lo))
+            nc.vector.tensor_copy(pair[:, 0:n], h[i][:].indirect(pos1_sb[:, lo // 16 : hi // 16]))
+            nc.vector.tensor_copy(pair[:, n : 2 * n], h[i][:].indirect(pos2_sb[:, lo // 16 : hi // 16]))
+            pairs[i, lo] = pair
 
-        def add_pairs(g, t, lo, hi, pair):
+        def square_add(i, lo, hi):
             n = hi - lo
-            nc.gpsimd.tensor_tensor(zsum[g][:, t, lo:hi], pair[:, 0:n], pair[:, n : 2 * n], ALU.add)
+            pair = pairs[i, lo]
+            nc.scalar.activation(pair[:, 0 : 2 * n], pair[:, 0 : 2 * n], ACT.Square)
+            nc.vector.tensor_tensor(zsum[i // PACK][:, i % PACK, lo:hi], pair[:, 0:n], pair[:, n : 2 * n], ALU.add)
 
-        def root(g, lo, hi):
+        def root_quant(g, lo, hi):
             nc.scalar.activation(
                 zb[g][:, lo:hi, :].rearrange("p (c i) t -> p c t i", i=4),
                 zsum[g][:, :, lo:hi].rearrange("p t (c i) -> p c t i", i=4),
                 ACT.Sqrt,
             )
-
-        def quant_z(g, lo, hi):
             nc.vector.quantize_mx(
                 out=zq[g][:, lo:hi].bitcast(FP8X4), scales=zs[g][:, lo:hi], in_=zb[g][:, lo:hi, :].rearrange("p m t -> p (m t)")
             )
 
-        y = [big([P, PACK, S], F32, "y%d" % g) for g in range(GROUPS)]
-
         def scale_h(i):
-            nc.gpsimd.tensor_scalar(y[i // PACK][:, i % PACK, :], h[i][:], gh_sb[:, i // PACK, i % PACK : i % PACK + 1], 0.0, ALU.mult, ALU.add)
+            cols = pool_cols[i]
+            if cols > 0:
+                nc.vector.tensor_scalar(
+                    y[i // PACK][:, i % PACK, 0:cols], h[i][:, 0:cols], gh_sb[:, i // PACK, i % PACK : i % PACK + 1], 0.0, ALU.mult, ALU.add
+                )
 
-        on_pool = [0,1,2,3,4,5]
-        steps = [(0, t, 0, M) for t in range(PACK)] + [(1, 0, 0, M), (1, 1, 0, M)] + [(1, 2, 0, 256), (1, 3, 0, 256), (1, 2, 256, M), (1, 3, 256, M)]
-        w_split = [0, 32, 64]
-        def finish_pairs(g, t, lo, hi, pair):
-            nc.scalar.activation(pair[:, 0 : 2 * (hi - lo)], pair[:, 0 : 2 * (hi - lo)], ACT.Square)
-            add_pairs(g, t, lo, hi, pair)
-            if t == PACK - 1:
-                for c in range(lo, hi, 256):
-                    root(g, c, min(hi, c + 256))
-                    quant_z(g, c, min(hi, c + 256))
+        evacuate_h(0)
+        evacuate_h(1)
+        for a in range(PASSES):
+            pick_pairs(a, 0, M)
+            quant_w1(1, a, raws[a], (0, 0, 128)[a])
+            if a + 2 < PACK:
+                evacuate_h(a + 2)
+        pick_pairs(3, 0, M)
+        square_add(0, 0, M)
+        square_add(1, 0, M)
+        evacuate_h(4)
+        pick_pairs(4, 0, M)
+        square_add(2, 0, M)
+        evacuate_h(5)
+        pick_pairs(5, 0, M)
+        square_add(3, 0, M)
+        evacuate_h(6)
+        evacuate_h(7)
+        root_quant(0, 0, 512)
+        square_add(4, 0, M)
 
-        lag = 1
-        ahead = 1
-        picks = []
-        ready = 0
-        for n, (g, t, lo, hi) in enumerate(steps):
-            while ready < min(TILES, n + ahead + 1):
-                if ready >= PACK:
-                    for half in range(2):
-                        accs[ready % PACK, half] = bank("acc1%d%d" % (ready % PACK, half))
-                        for a in range(PASSES):
-                            stage1_pass(accs[ready % PACK, half], 1, ready % PACK, a, half)
-                evacuate_h(ready // PACK, ready % PACK)
-
-                ready = ready + 1
-            picks.append((g, t, lo, hi, pick_pairs(g, t, lo, hi)))
-            if n < PASSES:
-                quant_w1(1, n, round_w1(1, n, raws[n], w_split[n]))
-            if n >= lag:
-                finish_pairs(*picks[n - lag])
-            if n in on_pool:
-                scale_h(n)
-            if n in [5, 6]:
-                deal_w4([5, 6].index(n))
-
-        for item in picks[len(steps) - lag :]:
-            finish_pairs(*item)
+        cuts = (0, 256, M)
+        tail = [(i, lo, hi) for lo, hi in zip(cuts[:-1], cuts[1:]) for i in (TILES - 2, TILES - 1)]
+        pick_pairs(*tail[0])
+        square_add(5, 0, M)
+        pick_pairs(*tail[1])
+        for n, (i, lo, hi) in enumerate(tail):
+            if n + 2 < len(tail):
+                pick_pairs(*tail[n + 2])
+            square_add(i, lo, hi)
+            if i == TILES - 1:
+                root_quant(1, lo, hi)
+        for i in range(TILES):
+            scale_h(i)
         nc.scalar.activation(warm[:, 2:3], zb[1][:, M - 1, 0:1], ACT.Silu)
 
-        bt = keep.tile([P, TILES * M], F32, name="bt", align_bytes=64)
+        bt = held([P, TILES * M], F32, "bt")
 
         def stage2(i):
-            acc = bank("acc2%d" % i)
-            pieces = [(0, 0, M)] + ([(1, c, c + P) for c in range(0, M, P)] if i < 0 else [(1, 0, M)])
+            acc = bank("acc2_%d" % i)
+            pieces = [(0, 0, M)] + ([(1, c, c + P) for c in range(0, M, P)] if i < 1 else [(1, 0, M)])
             for k, (a, lo, hi) in enumerate(pieces):
                 nc.tensor.matmul_mx(
                     out=acc[:, lo:hi],
-                    lhsT=w4d[i // PACK][:, a, 2 * P * (i % PACK) : 2 * P * (i % PACK + 1)].bitcast(FP4X4),
-                    lhsT_scale=w4s[i // PACK][:, a, P * (i % PACK) : P * (i % PACK + 1)],
+                    lhsT=w4d[:, a, 2 * P * i : 2 * P * (i + 1)].bitcast(FP4X4),
+                    lhsT_scale=w4s[:, a, P * i : P * (i + 1)],
                     rhs=zq[a][:, lo:hi].bitcast(FP8X4),
                     rhs_scale=zs[a][:, lo:hi],
                     start=(k == 0),
                     stop=(k == len(pieces) - 1),
                 )
             base = (TILES - 1 - i) * M
-            if i == 0:
+            if i < 1:
                 nc.vector.tensor_copy(bt[:, base : base + M], acc[:])
             else:
                 nc.scalar.copy(bt[:, base : base + M], acc[:])
 
-        yq = [keep.tile([P, S], I32, name="yq%d" % g, align_bytes=64) for g in range(GROUPS)]
-        ys = [keep.tile([P, S], U8, name="ys%d" % g, align_bytes=64) for g in range(GROUPS)]
+        yq = [held([P, S], I32, "yq%d" % g) for g in range(GROUPS)]
+        ys = [held([P, S], U8, "ys%d" % g) for g in range(GROUPS)]
+        ups = {}
 
-        def pick_up(g, t, lo, hi):
-            i = PACK * g + t
+        def pick_up(i, lo, hi):
             base = (TILES - 1 - i) * M
-            up = picked("up%d%d%d" % (g, t, lo))
+            up = picked("up%d_%d" % (i, lo))
             piece = min(hi - lo, 256 << min(i, 2))
             width = max(M, 3 * piece // 2)
             for c in range(lo, hi, piece):
                 nc.vector.tensor_copy(
                     up[:, c - lo : c - lo + piece], bt[:, base : base + width].indirect(pos3_sb[:, c // 16 : (c + piece) // 16])
                 )
-            nc.scalar.activation(up[:, 0 : hi - lo], up[:, 0 : hi - lo], ACT.Silu)
-            return up
+            ups[i, lo] = up
 
-        def combine(g, t, lo, hi, up):
-            i = PACK * g + t
-            if i in on_pool:
-                nc.gpsimd.tensor_tensor(y[g][:, t, lo:hi], y[g][:, t, lo:hi], up[:, 0 : hi - lo], ALU.add)
+        def combine(i, lo, hi):
+            g, t = divmod(i, PACK)
+            up = ups[i, lo][:, 0 : hi - lo]
+            nc.scalar.activation(up, up, ACT.Silu)
+            if hi <= pool_cols[i]:
+                nc.gpsimd.tensor_tensor(y[g][:, t, lo:hi], y[g][:, t, lo:hi], up, ALU.add)
             else:
-                nc.vector.scalar_tensor_tensor(
-                    y[g][:, t, lo:hi], h[i][:, lo:hi], gh_sb[:, g, t : t + 1], up[:, 0 : hi - lo], ALU.mult, ALU.add
-                )
+                nc.vector.scalar_tensor_tensor(y[g][:, t, lo:hi], h[i][:, lo:hi], gh_sb[:, g, t : t + 1], up, ALU.mult, ALU.add)
 
-        def round_y(g, lo, hi, on_vector):
-            yb = keep.tile([P, hi - lo, PACK], BF16, name="yb%d%d" % (g, lo), tag="wg", bufs=3, align_bytes=64)
+        def finish_y(g, lo, hi, on_vector):
+            nc.sync.dma_start(out_0[g * KP : (g + 1) * KP, lo:hi].rearrange("(p t) c -> p t c", t=PACK), y[g][:, :, lo:hi])
+            yb = rounded([P, hi - lo, PACK], "yb%d_%d" % (g, lo))
             dst = yb[:].rearrange("p (c i) t -> p c t i", i=4)
             src = y[g][:, :, lo:hi].rearrange("p t (c i) -> p c t i", i=4)
             if on_vector:
                 nc.vector.tensor_copy(dst, src)
             else:
                 nc.scalar.copy(dst, src)
-            nc.sync.dma_start(out_0[g * KP : (g + 1) * KP, lo:hi].rearrange("(p t) c -> p t c", t=PACK), y[g][:, :, lo:hi])
-            return yb
-
-        def quant_y(g, lo, hi, yb):
             nc.vector.quantize_mx(
                 out=yq[g][:, lo:hi].bitcast(FP8X4), scales=ys[g][:, lo:hi], in_=yb[:].rearrange("p m t -> p (m t)")
             )
@@ -312,21 +314,25 @@ def tile_list_blast_window_features_kernel(
                 for q in range(4):
                     nc.sync.dma_start(out_2[g, 4 * q : 4 * q + 4, :].bitcast(I32), ys[g][32 * q : 32 * q + 4, :].bitcast(I32))
 
-        steps = [(g, t, lo, hi) for g, cuts in ((0, (0, 512, S)), (1, (0, 512, 768, S))) for lo, hi in zip(cuts[:-1], cuts[1:]) for t in range(PACK)]
-        stage2(0)
-
-        stage2(1)
-        pending = None
-        for n, (g, t, lo, hi) in enumerate(steps):
-            up = pick_up(g, t, lo, hi)
-            if n + 2 < TILES:
-                stage2(n + 2)
-            if pending is not None:
-                combine(*pending)
-                pg, pt, plo, phi = pending[:4]
-                if pt == PACK - 1:
-                    for c in range(plo, phi, 256):
-                        quant_y(pg, c, min(c + 256, phi), round_y(pg, c, min(c + 256, phi), False))
-            pending = (g, t, lo, hi, up)
-        combine(*pending)
-        quant_y(1, pending[2], S, round_y(1, pending[2], S, True))
+        steps = [(PACK * g + t, lo, hi) for g, cuts in ((0, (0, 512, S)), (1, (0, 512, 768, S))) for lo, hi in zip(cuts[:-1], cuts[1:]) for t in range(PACK)]
+        lag = 1
+        cast_lag = 4
+        width = 512
+        evacuated = 0
+        casts = []
+        for n in range(len(steps) + lag):
+            while evacuated < min(TILES, n + 2):
+                stage2(evacuated)
+                evacuated = evacuated + 1
+            if n < len(steps):
+                pick_up(*steps[n])
+            if n >= lag:
+                i, lo, hi = steps[n - lag]
+                combine(i, lo, hi)
+                if i % PACK == PACK - 1:
+                    casts = casts + [(n + cast_lag + k, i // PACK, c, min(c + width, hi)) for k, c in enumerate(range(lo, hi, width))]
+            while casts and casts[0][0] <= n:
+                finish_y(*casts[0][1:], False)
+                casts = casts[1:]
+        for k, item in enumerate(casts):
+            finish_y(*item[1:], k == len(casts) - 1)

@@ -147,7 +147,7 @@ def tile_list_blast_window_features_kernel(
             if a == 0:
                 nc.vector.tensor_copy(vs[:], ts[:].indirect(offs_sb[:]))
             if last:
-                quant_w1(0, a, raw, P // 2, (0, 1, 2, PACK))
+                quant_w1(0, a, raw, 44, (0, 1, 2, PACK))
             else:
                 quant_w1(0, a, raw, 0)
             if a == 0:
@@ -171,7 +171,7 @@ def tile_list_blast_window_features_kernel(
         zq = [held([P, M], U32, "zq%d" % g) for g in range(GROUPS)]
         zs = [held([P, M], U8, "zs%d" % g) for g in range(GROUPS)]
         y = [big([P, PACK, S], F32, "y%d" % g) for g in range(GROUPS)]
-        pool_cols = [0] * TILES
+        pool_cols = [S] * 4 + [0] * 4
 
         def evacuate_h(i):
             for half in range(2):
@@ -220,7 +220,7 @@ def tile_list_blast_window_features_kernel(
         evacuate_h(1)
         for a in range(PASSES):
             pick_pairs(a, 0, M)
-            quant_w1(1, a, raws[a], (0, 0, 128)[a])
+            quant_w1(1, a, raws[a], (0, 0, 96)[a])
             if a + 2 < PACK:
                 evacuate_h(a + 2)
         pick_pairs(3, 0, M)
@@ -234,8 +234,8 @@ def tile_list_blast_window_features_kernel(
         square_add(3, 0, M)
         evacuate_h(6)
         evacuate_h(7)
-        root_quant(0, 0, 512)
         square_add(4, 0, M)
+        root_quant(0, 0, 512)
 
         cuts = (0, 256, M)
         tail = [(i, lo, hi) for lo, hi in zip(cuts[:-1], cuts[1:]) for i in (TILES - 2, TILES - 1)]
@@ -247,9 +247,8 @@ def tile_list_blast_window_features_kernel(
                 pick_pairs(*tail[n + 2])
             square_add(i, lo, hi)
             if i == TILES - 1:
-                root_quant(1, lo, hi)
-        for i in range(TILES):
-            scale_h(i)
+                for c in range(lo, hi, P if hi == M else 2 * P):
+                    root_quant(1, c, c + (P if hi == M else 2 * P))
         nc.scalar.activation(warm[:, 2:3], zb[1][:, M - 1, 0:1], ACT.Silu)
 
         bt = held([P, TILES * M], F32, "bt")
@@ -290,22 +289,27 @@ def tile_list_blast_window_features_kernel(
 
         def combine(i, lo, hi):
             g, t = divmod(i, PACK)
-            up = ups[i, lo][:, 0 : hi - lo]
-            nc.scalar.activation(up, up, ACT.Silu)
-            if hi <= pool_cols[i]:
-                nc.gpsimd.tensor_tensor(y[g][:, t, lo:hi], y[g][:, t, lo:hi], up, ALU.add)
-            else:
-                nc.vector.scalar_tensor_tensor(y[g][:, t, lo:hi], h[i][:, lo:hi], gh_sb[:, g, t : t + 1], up, ALU.mult, ALU.add)
+            cut = max(lo, min(hi, pool_cols[i]))
+            if cut > lo:
+                up = ups[i, lo][:, 0 : cut - lo]
+                nc.scalar.activation(y[g][:, t, lo:cut], h[i][:, lo:cut], ACT.Copy, scale=gh_sb[:, g, t : t + 1])
+                nc.scalar.activation(up, up, ACT.Silu)
+                for c in range(lo, cut, 256):
+                    nc.gpsimd.tensor_tensor(y[g][:, t, c : c + 256], y[g][:, t, c : c + 256], up[:, c - lo : c - lo + 256], ALU.add)
+            if cut < hi:
+                up = ups[i, lo][:, cut - lo : hi - lo]
+                nc.scalar.activation(up, up, ACT.Silu)
+                nc.vector.scalar_tensor_tensor(y[g][:, t, cut:hi], h[i][:, cut:hi], gh_sb[:, g, t : t + 1], up, ALU.mult, ALU.add)
 
         def finish_y(g, lo, hi, on_vector):
             nc.sync.dma_start(out_0[g * KP : (g + 1) * KP, lo:hi].rearrange("(p t) c -> p t c", t=PACK), y[g][:, :, lo:hi])
             yb = rounded([P, hi - lo, PACK], "yb%d_%d" % (g, lo))
             dst = yb[:].rearrange("p (c i) t -> p c t i", i=4)
             src = y[g][:, :, lo:hi].rearrange("p t (c i) -> p c t i", i=4)
-            if on_vector:
-                nc.vector.tensor_copy(dst, src)
-            else:
-                nc.scalar.copy(dst, src)
+            cut = 40 if on_vector else 0
+            if cut > 0:
+                nc.vector.tensor_copy(dst[:, 0:cut], src[:, 0:cut])
+            nc.scalar.copy(dst[:, cut:], src[:, cut:])
             nc.vector.quantize_mx(
                 out=yq[g][:, lo:hi].bitcast(FP8X4), scales=ys[g][:, lo:hi], in_=yb[:].rearrange("p m t -> p (m t)")
             )
@@ -316,7 +320,7 @@ def tile_list_blast_window_features_kernel(
 
         steps = [(PACK * g + t, lo, hi) for g, cuts in ((0, (0, 512, S)), (1, (0, 512, 768, S))) for lo, hi in zip(cuts[:-1], cuts[1:]) for t in range(PACK)]
         lag = 1
-        cast_lag = 4
+        cast_lag = 5
         width = 512
         evacuated = 0
         casts = []

from contextlib import ExitStack

import concourse.mybir as mybir

K, T, S, M, H = 1536, 4096, 1024, 512, 1024
FLOPS = 2 * K * H * S + 2 * H * H * M

F32 = mybir.dt.float32
BF16 = mybir.dt.bfloat16
I32 = mybir.dt.int32
U32 = mybir.dt.uint32
U16 = mybir.dt.uint16
U8 = mybir.dt.uint8
FP8X4 = mybir.dt.float8_e4m3fn_x4
FP4X4 = mybir.dt.float4_e2m1fn_x4
ACT = mybir.ActivationFunctionType
ALU = mybir.AluOpType

P = 128
PACK = 4
KP = P * PACK
BANK = 512
PASSES = K // KP
GROUPS = H // KP
TILES = GROUPS * PACK


def tile_list_blast_window_features_kernel(
    tc, tab_words, tab_scales, offs, w1, pos1, pos2, w4_words, w4_scales, pos3, gh, out_0, out_1, out_2
):
    nc = tc.nc
    with ExitStack() as ctx:
        lists = ctx.enter_context(tc.tile_pool(name="lists", bufs=1))
        keep = ctx.enter_context(tc.tile_pool(name="keep", bufs=1))
        psum = ctx.enter_context(tc.psum_pool(name="psum", bufs=8))

        def held(shape, dtype, name):
            return keep.tile(shape, dtype, name=name, align_bytes=64)

        def big(shape, dtype, name):
            return keep.tile(shape, dtype, name=name, tag="big", bufs=3, align_bytes=64)

        def rounded(shape, name):
            return keep.tile(shape, BF16, name=name, tag="rounded", bufs=3, align_bytes=64)

        def picked(name):
            return keep.tile([P, S], F32, name=name, tag="picked", bufs=8, align_bytes=64)

        def bank(name):
            return psum.tile([P, BANK], F32, name=name, tag="bank")

        offs_sb = lists.tile([P, S // 16], U16, name="offs_sb")
        pos1_sb = lists.tile([P, M // 16], U16, name="pos1_sb")
        pos2_sb = lists.tile([P, M // 16], U16, name="pos2_sb")
        pos3_sb = lists.tile([P, S // 16], U16, name="pos3_sb")
        gh_sb = lists.tile([P, GROUPS, PACK], F32, name="gh_sb")
        warm = lists.tile([P, 8], F32, name="warm")

        nc.vector.memset(warm[:], 1.0)
        nc.scalar.activation(warm[:, 0:1], warm[:, 1:2], ACT.Sqrt)

        ts = held([P, T], U8, "ts")
        nc.vector.memset(ts[:].bitcast(I32), 0)
        w4sraw = held([P, GROUPS, H], U8, "w4sraw")
        nc.vector.memset(w4sraw[:].bitcast(I32), 0)
        for q in range(4):
            nc.gpsimd.dma_start(
                ts[32 * q : 32 * q + 4 * PASSES, :].bitcast(I32), tab_scales[:, 4 * q : 4 * q + 4, :].bitcast(I32)
            )

        def load_table(a):
            tw = big([P, T], I32, "tw%d" % a)
            nc.sync.dma_start(tw[:], tab_words[a].rearrange("p t i -> p (t i)").bitcast(I32))
            return tw

        def load_w1(g, a, pieces=1):
            raw = big([P, PACK, KP], F32, "wraw%d%d" % (g, a))
            src = w1[a * KP : (a + 1) * KP, g * KP : (g + 1) * KP].rearrange("(p j) c -> p j c", j=PACK)
            for c in range(0, KP, KP // pieces):
                nc.sync.dma_start(raw[:, :, c : c + KP // pieces], src[:, :, c : c + KP // pieces])
            return raw

        wq = {}
        ws = {}

        def quant_w1(g, a, raw, on_vector, cuts=(0, PACK)):
            grouped = rounded([P, PACK, P, PACK], "wg%d%d" % (g, a))
            src = raw[:].rearrange("p j (m t) -> p m j t", t=PACK)
            dst = grouped[:].rearrange("p t m j -> p m j t")
            for c in range(0, P - on_vector, 32):
                hi = min(c + 32, P - on_vector)
                nc.scalar.copy(dst[:, c:hi], src[:, c:hi])
            if on_vector > 0:
                nc.vector.tensor_copy(dst[:, P - on_vector : P], src[:, P - on_vector : P])
            wq[g, a] = held([P, KP], U32, "wq%d%d" % (g, a))
            ws[g, a] = held([P, KP], U8, "ws%d%d" % (g, a))
            for lo, hi in zip(cuts[:-1], cuts[1:]):
                nc.vector.quantize_mx(
                    out=wq[g, a][:, lo * P : hi * P].bitcast(FP8X4),
                    scales=ws[g, a][:, lo * P : hi * P],
                    in_=grouped[:, lo:hi].rearrange("p t m j -> p (t m j)"),
                )

        v = [held([P, S], U32, "v%d" % a) for a in range(PASSES)]
        vs = held([P, S], U8, "vs")
        accs = {}

        def stage1_pass(i, a, half):
            g, t = divmod(i, PACK)
            if a == 0:
                accs[i, half] = bank("acc1_%d%d" % (i, half))
            cols = slice(half * BANK, (half + 1) * BANK)
            rows = slice(t * P, (t + 1) * P)
            nc.tensor.matmul_mx(
                out=accs[i, half][:],
                lhsT=wq[g, a][:, rows].bitcast(FP8X4),
                lhsT_scale=ws[g, a][:, rows],
                rhs=v[a][:, cols].bitcast(FP8X4),
                rhs_scale=vs[4 * a :, cols],
                start=(a == 0),
                stop=(a == PASSES - 1),
            )

        w4raw = held([P, GROUPS, 2 * H], U8, "w4raw")
        w4d = held([P, GROUPS, 2 * H], U8, "w4d")
        w4s = held([P, GROUPS, H], U8, "w4s")

        for a in range(PASSES):
            tw = load_table(a)
            if a == 0:
                nc.sync.dma_start(offs_sb[:], offs)
            if a == 1:
                for q in range(4):
                    nc.sync.dma_start(
                        w4sraw[32 * q : 32 * q + 4].bitcast(I32),
                        w4_scales[:, 4 * q : 4 * q + 4, :].rearrange("a r c -> r a c").bitcast(I32),
                    )
            last = a == PASSES - 1
            raw = load_w1(0, a, 2 if last else 1)
            if a == 0:
                nc.sync.dma_start(w4raw[:].bitcast(I32), w4_words.rearrange("a p c -> p a c").bitcast(I32))
                nc.sync.dma_start(pos1_sb[:], pos1)
                nc.sync.dma_start(pos2_sb[:], pos2)
                nc.sync.dma_start(pos3_sb[:], pos3)
                nc.sync.dma_start(gh_sb[:], gh.rearrange("(g p t) -> p g t", g=GROUPS, t=PACK))
            nc.vector.tensor_copy(v[a][:], tw[:].bitcast(U32).indirect(offs_sb[:]))
            if a == 0:
                nc.vector.tensor_copy(vs[:], ts[:].indirect(offs_sb[:]))
            if last:
                quant_w1(0, a, raw, 44, (0, 1, 2, PACK))
            else:
                quant_w1(0, a, raw, 0)
            if a == 0:
                nc.vector.tensor_copy(
                    w4d[:].bitcast(U16).rearrange("p a (g t q) -> p (a g) q t", g=GROUPS, t=PACK),
                    w4raw[:].bitcast(U16).rearrange("p a (g q t) -> p (a g) q t", g=GROUPS, t=PACK),
                )
            if a == 1:
                nc.vector.tensor_copy(
                    w4s[:].rearrange("p a (g t q) -> p (a g) q t", g=GROUPS, t=PACK),
                    w4sraw[:].rearrange("p a (g q t) -> p (a g) q t", g=GROUPS, t=PACK),
                )
            for i in range(PACK):
                for half in range(2):
                    stage1_pass(i, a, half)
        raws = [load_w1(1, a) for a in range(PASSES)]

        h = [held([P, S], F32, "h%d" % i) for i in range(TILES)]
        zsum = [held([P, PACK, M], F32, "zsum%d" % g) for g in range(GROUPS)]
        zb = [held([P, M, PACK], BF16, "zb%d" % g) for g in range(GROUPS)]
        zq = [held([P, M], U32, "zq%d" % g) for g in range(GROUPS)]
        zs = [held([P, M], U8, "zs%d" % g) for g in range(GROUPS)]
        y = [big([P, PACK, S], F32, "y%d" % g) for g in range(GROUPS)]
        pool_cols = [S] * 4 + [0] * 4

        def evacuate_h(i):
            for half in range(2):
                if i >= PACK:
                    for a in range(PASSES):
                        stage1_pass(i, a, half)
                dst = h[i][:, half * BANK : (half + 1) * BANK]
                if (i, half) == (0, 1):
                    nc.vector.tensor_copy(dst, accs[i, half][:])
                else:
                    nc.scalar.copy(dst, accs[i, half][:])

        pairs = {}

        def pick_pairs(i, lo, hi):
            n = hi - lo
            pair = picked("pair%d_%d" % (i, lo))
            nc.vector.tensor_copy(pair[:, 0:n], h[i][:].indirect(pos1_sb[:, lo // 16 : hi // 16]))
            nc.vector.tensor_copy(pair[:, n : 2 * n], h[i][:].indirect(pos2_sb[:, lo // 16 : hi // 16]))
            pairs[i, lo] = pair

        def square_add(i, lo, hi):
            n = hi - lo
            pair = pairs[i, lo]
            nc.scalar.activation(pair[:, 0 : 2 * n], pair[:, 0 : 2 * n], ACT.Square)
            nc.vector.tensor_tensor(zsum[i // PACK][:, i % PACK, lo:hi], pair[:, 0:n], pair[:, n : 2 * n], ALU.add)

        def root_quant(g, lo, hi):
            nc.scalar.activation(
                zb[g][:, lo:hi, :].rearrange("p (c i) t -> p c t i", i=4),
                zsum[g][:, :, lo:hi].rearrange("p t (c i) -> p c t i", i=4),
                ACT.Sqrt,
            )
            nc.vector.quantize_mx(
                out=zq[g][:, lo:hi].bitcast(FP8X4), scales=zs[g][:, lo:hi], in_=zb[g][:, lo:hi, :].rearrange("p m t -> p (m t)")
            )

        def scale_h(i):
            cols = pool_cols[i]
            if cols > 0:
                nc.vector.tensor_scalar(
                    y[i // PACK][:, i % PACK, 0:cols], h[i][:, 0:cols], gh_sb[:, i // PACK, i % PACK : i % PACK + 1], 0.0, ALU.mult, ALU.add
                )

        evacuate_h(0)
        evacuate_h(1)
        for a in range(PASSES):
            pick_pairs(a, 0, M)
            quant_w1(1, a, raws[a], (0, 0, 96)[a])
            if a + 2 < PACK:
                evacuate_h(a + 2)
        pick_pairs(3, 0, M)
        square_add(0, 0, M)
        square_add(1, 0, M)
        evacuate_h(4)
        pick_pairs(4, 0, M)
        square_add(2, 0, M)
        evacuate_h(5)
        pick_pairs(5, 0, M)
        square_add(3, 0, M)
        evacuate_h(6)
        evacuate_h(7)
        square_add(4, 0, M)
        root_quant(0, 0, 512)

        cuts = (0, 256, M)
        tail = [(i, lo, hi) for lo, hi in zip(cuts[:-1], cuts[1:]) for i in (TILES - 2, TILES - 1)]
        pick_pairs(*tail[0])
        square_add(5, 0, M)
        pick_pairs(*tail[1])
        for n, (i, lo, hi) in enumerate(tail):
            if n + 2 < len(tail):
                pick_pairs(*tail[n + 2])
            square_add(i, lo, hi)
            if i == TILES - 1:
                for c in range(lo, hi, P if hi == M else 2 * P):
                    root_quant(1, c, c + (P if hi == M else 2 * P))
        nc.scalar.activation(warm[:, 2:3], zb[1][:, M - 1, 0:1], ACT.Silu)

        bt = held([P, TILES * M], F32, "bt")

        def stage2(i):
            acc = bank("acc2_%d" % i)
            pieces = [(0, 0, M)] + ([(1, c, c + P) for c in range(0, M, P)] if i < 1 else [(1, 0, M)])
            for k, (a, lo, hi) in enumerate(pieces):
                nc.tensor.matmul_mx(
                    out=acc[:, lo:hi],
                    lhsT=w4d[:, a, 2 * P * i : 2 * P * (i + 1)].bitcast(FP4X4),
                    lhsT_scale=w4s[:, a, P * i : P * (i + 1)],
                    rhs=zq[a][:, lo:hi].bitcast(FP8X4),
                    rhs_scale=zs[a][:, lo:hi],
                    start=(k == 0),
                    stop=(k == len(pieces) - 1),
                )
            base = (TILES - 1 - i) * M
            if i < 1:
                nc.vector.tensor_copy(bt[:, base : base + M], acc[:])
            else:
                nc.scalar.copy(bt[:, base : base + M], acc[:])

        yq = [held([P, S], I32, "yq%d" % g) for g in range(GROUPS)]
        ys = [held([P, S], U8, "ys%d" % g) for g in range(GROUPS)]
        ups = {}

        def pick_up(i, lo, hi):
            base = (TILES - 1 - i) * M
            up = picked("up%d_%d" % (i, lo))
            piece = min(hi - lo, 256 << min(i, 2))
            width = max(M, 3 * piece // 2)
            for c in range(lo, hi, piece):
                nc.vector.tensor_copy(
                    up[:, c - lo : c - lo + piece], bt[:, base : base + width].indirect(pos3_sb[:, c // 16 : (c + piece) // 16])
                )
            ups[i, lo] = up

        def combine(i, lo, hi):
            g, t = divmod(i, PACK)
            cut = max(lo, min(hi, pool_cols[i]))
            if cut > lo:
                up = ups[i, lo][:, 0 : cut - lo]
                nc.scalar.activation(y[g][:, t, lo:cut], h[i][:, lo:cut], ACT.Copy, scale=gh_sb[:, g, t : t + 1])
                nc.scalar.activation(up, up, ACT.Silu)
                for c in range(lo, cut, 256):
                    nc.gpsimd.tensor_tensor(y[g][:, t, c : c + 256], y[g][:, t, c : c + 256], up[:, c - lo : c - lo + 256], ALU.add)
            if cut < hi:
                up = ups[i, lo][:, cut - lo : hi - lo]
                nc.scalar.activation(up, up, ACT.Silu)
                nc.vector.scalar_tensor_tensor(y[g][:, t, cut:hi], h[i][:, cut:hi], gh_sb[:, g, t : t + 1], up, ALU.mult, ALU.add)

        def finish_y(g, lo, hi, on_vector):
            nc.sync.dma_start(out_0[g * KP : (g + 1) * KP, lo:hi].rearrange("(p t) c -> p t c", t=PACK), y[g][:, :, lo:hi])
            yb = rounded([P, hi - lo, PACK], "yb%d_%d" % (g, lo))
            dst = yb[:].rearrange("p (c i) t -> p c t i", i=4)
            src = y[g][:, :, lo:hi].rearrange("p t (c i) -> p c t i", i=4)
            cut = 40 if on_vector else 0
            if cut > 0:
                nc.vector.tensor_copy(dst[:, 0:cut], src[:, 0:cut])
            nc.scalar.copy(dst[:, cut:], src[:, cut:])
            nc.vector.quantize_mx(
                out=yq[g][:, lo:hi].bitcast(FP8X4), scales=ys[g][:, lo:hi], in_=yb[:].rearrange("p m t -> p (m t)")
            )
            nc.sync.dma_start(out_1[g].rearrange("p m t -> p (m t)").bitcast(I32)[:, lo:hi], yq[g][:, lo:hi])
            if hi == S:
                for q in range(4):
                    nc.sync.dma_start(out_2[g, 4 * q : 4 * q + 4, :].bitcast(I32), ys[g][32 * q : 32 * q + 4, :].bitcast(I32))

        steps = [(PACK * g + t, lo, hi) for g, cuts in ((0, (0, 512, S)), (1, (0, 512, 768, S))) for lo, hi in zip(cuts[:-1], cuts[1:]) for t in range(PACK)]
        lag = 1
        cast_lag = 5
        width = 512
        evacuated = 0
        casts = []
        for n in range(len(steps) + lag):
            while evacuated < min(TILES, n + 2):
                stage2(evacuated)
                evacuated = evacuated + 1
            if n < len(steps):
                pick_up(*steps[n])
            if n >= lag:
                i, lo, hi = steps[n - lag]
                combine(i, lo, hi)
                if i % PACK == PACK - 1:
                    casts = casts + [(n + cast_lag + k, i // PACK, c, min(c + width, hi)) for k, c in enumerate(range(lo, hi, width))]
            while casts and casts[0][0] <= n:
                finish_y(*casts[0][1:], False)
                casts = casts[1:]
        for k, item in enumerate(casts):
            finish_y(*item[1:], k == len(casts) - 1)
